import numpy as np
import ml_dtypes


def mxq(x, axis, fmt="e4m3"):
    dtype, down = {"e4m3": (ml_dtypes.float8_e4m3fn, 7), "e5m2": (ml_dtypes.float8_e5m2, 14)}[fmt]
    v = np.moveaxis(np.asarray(x, np.float32).astype(ml_dtypes.bfloat16).astype(np.float64), axis, -1)
    blocks = v.reshape(v.shape[:-1] + (-1, 32))
    amax = np.abs(blocks).max(-1, keepdims=True)
    byte = np.maximum(np.where(amax > 0, np.frexp(amax)[1] - 1 + 127, 0) - down, 1)
    scale = np.exp2(byte - 127.0)
    codes = (blocks / scale).astype(np.float32).astype(dtype).astype(np.float64)
    return np.moveaxis((codes * scale).reshape(v.shape), -1, axis)


WIDE = False


def mx_kscale(k):
    if not WIDE:
        return np.ones(k)
    levels = np.array([10, -10, 5, -5, 0])
    if k % 512:
        return np.exp2(np.random.permutation(np.resize(levels, k // 32))).repeat(32)
    a = np.empty((k // 512, 16))
    for p in range(k // 512):
        a[p, :8] = np.random.permutation(np.resize(levels, 8))
        for g in range(8):
            far = levels[np.abs(levels - a[p, g]) >= 10]
            a[p, g + 8] = far[np.random.randint(len(far))]
    return np.exp2(a.ravel()).repeat(32)


def f64(x):
    return np.asarray(x).astype(np.float64)


def striped(idx):
    return np.tile(idx.reshape(-1, 16).T, (8, 1)).astype(np.uint16)


def unstriped(offs):
    return offs[:16].T.reshape(-1).astype(np.int64)


E2M1 = np.array([0.0, 0.5, 1.0, 1.5, 2.0, 3.0, 4.0, 6.0, -0.0, -0.5, -1.0, -1.5, -2.0, -3.0, -4.0, -6.0])


def pack_weight(w, fmt):
    k, n = w.shape
    w = f64(np.asarray(w, np.float32).astype(ml_dtypes.bfloat16)).reshape(k // 32, 32, n)
    amax = np.abs(w).max(1)
    if fmt == "e4m3":
        byte = np.frexp(amax)[1] - 1 + 127 - 7
    else:
        mant, ex = np.frexp(amax / 6.0)
        byte = np.where(mant > 0.5, ex, ex - 1) + 127
    byte = np.clip(np.where(amax > 0, byte, 1), 1, 254)
    scaled = (w * np.exp2(127.0 - byte)[:, None, :]).reshape(k, n).astype(np.float32)
    by_word = np.ascontiguousarray(scaled.reshape(k // 512, 128, 4, n).transpose(0, 1, 3, 2))
    if fmt == "e4m3":
        words = by_word.astype(ml_dtypes.float8_e4m3fn).view(np.uint8)
    else:
        c = by_word.astype(ml_dtypes.float4_e2m1fn).view(np.uint8) & 0xF
        words = (c[..., 0::2] | (c[..., 1::2] << 4)).reshape(k // 512, 128, 2 * n)
    return np.ascontiguousarray(words), np.ascontiguousarray(byte.astype(np.uint8).reshape(k // 512, 16, n))


def unpack_weight(words, scales, fmt):
    g, _, n = scales.shape
    words = np.ascontiguousarray(words).reshape(g, 128, n, -1)
    if fmt == "e4m3":
        vals = words.view(ml_dtypes.float8_e4m3fn).astype(np.float64)
    else:
        nib = np.empty((g, 128, n, 4), np.uint8)
        nib[..., 0::2] = words & 0xF
        nib[..., 1::2] = words >> 4
        vals = E2M1[nib]
    vals = vals * np.repeat(np.exp2(scales.astype(np.float64) - 127.0), 8, axis=1)[..., None]
    return vals.transpose(0, 1, 3, 2).reshape(g * 512, n)


def pack_table(v):
    words, scales = pack_weight(v, "e4m3")
    return np.concatenate([words.reshape(words.shape[0], -1), scales.reshape(scales.shape[0], -1)], axis=1)


def unpack_table(tab):
    g, t = tab.shape[0], tab.shape[1] // 528
    return unpack_weight(tab[:, :512 * t].reshape(g, 128, t, 4), tab[:, 512 * t:].reshape(g, 16, t), "e4m3")


def silu(v):
    return v / (1.0 + np.exp(-np.maximum(v, -700.0)))


G, K, M, T, S = 2, 1024, 512, 2048, 512


def setup_inputs():
    n = np.random.standard_normal
    s = mx_kscale(K)[:, None]
    return {
        "tab": pack_table(n((K, T)) * s),
        "w": (n((K, M)) / np.sqrt(K) / s).astype(np.float32),
        "b": (0.3 * n(512)).astype(np.float32),
        "offs": striped(np.concatenate([np.random.permutation(T)[:S] for _ in range(G)])),
    }


def reference(tab, w, b, offs):
    tab_ = unpack_table(tab)[:, unstriped(offs).reshape(G, S)].sum(1)
    w_ = mxq(f64(w), 0, "e4m3")
    y = w_.T @ tab_
    return silu(y + f64(b)[:, None])

@@ -1,0 +1,185 @@
+from contextlib import ExitStack
+
+import concourse.mybir as mybir
+
+G, K, M, T, S = 2, 1024, 512, 2048, 512
+FLOPS = 2 * G * K * M * S
+
+F32 = mybir.dt.float32
+BF16 = mybir.dt.bfloat16
+I32 = mybir.dt.int32
+U32 = mybir.dt.uint32
+U16 = mybir.dt.uint16
+U8 = mybir.dt.uint8
+FP8X4 = mybir.dt.float8_e4m3fn_x4
+SILU = mybir.ActivationFunctionType.Silu
+
+P = 128
+PACK = 4
+K_PASS = P * PACK
+PASSES = K // K_PASS
+TILES = M // P
+LIST_COLS = S // 16
+HALF = S // 2
+
+
+def tile_list_tabbag_silu_kernel(tc, tab, w, b, offs, out):
+    nc = tc.nc
+    with ExitStack() as ctx:
+        keep = ctx.enter_context(tc.tile_pool(name="keep", bufs=1))
+        psum = ctx.enter_context(tc.psum_pool(name="psum", bufs=1))
+
+        offsets = keep.tile([P, G * LIST_COLS], U16, name="offsets")
+        nc.sync.dma_start(offsets[:], offs)
+
+        plane = keep.tile([P, T // 4], I32, name="plane", tag="slot_plane", align_bytes=64)
+        nc.vector.memset(plane[:], 0)
+        for q in range(4):
+            lo = K_PASS * T + 4 * q * T
+            nc.scalar.dma_start(
+                plane[32 * q : 32 * q + 4 * PASSES, :],
+                tab[:, lo : lo + 4 * T].rearrange("a (r c) -> a r c", r=4).bitcast(I32),
+            )
+
+        warm_in = keep.tile([P, 1], F32, name="warm_in")
+        warm_out = keep.tile([P, 1], F32, name="warm_out")
+        nc.vector.memset(warm_in[:], 0.0)
+        nc.scalar.activation(warm_out[:], warm_in[:], SILU)
+
+        words = {}
+        raw = {}
+        bias = keep.tile([P, TILES], F32, name="bias")
+
+        def load_words(a):
+            wt = keep.tile([P, T], I32, name="words%d" % a, align_bytes=64)
+            nc.sync.dma_start(wt[:], tab[a, 0 : K_PASS * T].rearrange("(p c) -> p c", p=P).bitcast(I32))
+            words[a] = wt
+
+        def load_w(a, m0, n):
+            rt = keep.tile([P, PACK, n * P], F32, name="raw%d_%d" % (a, m0), align_bytes=64)
+            rows = w[a * K_PASS : (a + 1) * K_PASS, m0 * P : (m0 + n) * P]
+            nc.sync.dma_start(rt[:], rows.rearrange("(p j) c -> p j c", j=PACK))
+            for i in range(n):
+                raw[(a, m0 + i)] = rt[:, :, i * P : (i + 1) * P]
+
+        def load_bias():
+            with nc.allow_non_contiguous_dma(reason="one bias value a partition"):
+                nc.sync.dma_start(bias[:], b.rearrange("(m p) -> p m", p=P))
+
+        load_words(0)
+        load_w(0, 0, 1)
+        load_words(1)
+        load_bias()
+        load_w(0, 1, 1)
+        load_w(0, 2, 1)
+        load_w(0, 3, 1)
+        load_w(1, 0, 1)
+        load_w(1, 1, 1)
+        load_w(1, 2, 1)
+        load_w(1, 3, 1)
+
+        picked_scales = {}
+        picked = {}
+        grouped = {}
+        codes = {}
+        scales = {}
+        acc = {}
+        for m in range(TILES - 1):
+            acc[(m, 0)] = psum.tile([P, S], F32, name="acc%d" % m)
+        for lo in (0, HALF):
+            acc[(TILES - 1, lo)] = psum.tile([P, HALF], F32, name="acc_last%d" % lo)
+
+        def gather_scales():
+            t = keep.tile([P, G * S], U8, name="ps", align_bytes=64)
+            nc.vector.tensor_copy(t[:], plane[:].bitcast(U8).indirect(offsets[:]))
+            picked_scales[0] = t
+
+        def gather_both(a, tag):
+            t = keep.tile([P, G * S], U32, name="pw%d" % a, tag=tag, align_bytes=64)
+            nc.vector.tensor_copy(t[:], words[a][:].bitcast(U32).indirect(offsets[:]))
+            for g in range(G):
+                picked[(a, g)] = [(0, S, t[:, g * S : (g + 1) * S])]
+
+        def gather_words(a, g, lo, n, tag):
+            t = keep.tile([P, n], U32, name="pw%d_%d_%d" % (a, g, lo), tag=tag, align_bytes=64)
+            c0 = g * LIST_COLS + lo // 16
+            nc.vector.tensor_copy(t[:], words[a][:].bitcast(U32).indirect(offsets[:, c0 : c0 + n // 16]))
+            picked.setdefault((a, g), []).append((lo, n, t[:]))
+
+        def interleave(a, m, on_scalar, tag):
+            t = keep.tile([P, P, PACK], BF16, name="gr%d_%d" % (a, m), tag=tag, align_bytes=64)
+            dst = t[:].rearrange("p (c i) j -> p c j i", i=4)
+            src = raw[(a, m)].rearrange("p j (c i) -> p c j i", i=4)
+            if on_scalar:
+                nc.scalar.copy(dst, src)
+            else:
+                nc.vector.tensor_copy(dst, src)
+            grouped[(a, m)] = t
+
+        def quantize(a, m):
+            c = keep.tile([P, P], U32, name="wc%d_%d" % (a, m), align_bytes=64)
+            s = keep.tile([P, P], U8, name="ws%d_%d" % (a, m), align_bytes=64)
+            nc.vector.quantize_mx(
+                out=c[:].bitcast(FP8X4), scales=s[:], in_=grouped[(a, m)][:].rearrange("p c j -> p (c j)")
+            )
+            codes[(a, m)] = c
+            scales[(a, m)] = s
+
+        def spans(m):
+            return [(0, S)] if m < TILES - 1 else [(0, HALF), (HALF, HALF)]
+
+        def multiply(a, m, g, s0, sn):
+            parts = []
+            for lo, n, t in picked[(a, g)]:
+                x0, x1 = max(lo, s0), min(lo + n, s0 + sn)
+                if x1 > x0:
+                    parts.append((x0, x1, t[:, x0 - lo : x1 - lo]))
+            for i, (x0, x1, rhs) in enumerate(parts):
+                nc.tensor.matmul_mx(
+                    out=acc[(m, s0)][:, x0 - s0 : x1 - s0],
+                    lhsT=codes[(a, m)][:].bitcast(FP8X4),
+                    lhsT_scale=scales[(a, m)][:],
+                    rhs=rhs.bitcast(FP8X4),
+                    rhs_scale=picked_scales[0][4 * a : P, g * S + x0 : g * S + x1],
+                    start=(a == 0 and g == 0),
+                    stop=(a == PASSES - 1 and g == G - 1 and i == len(parts) - 1),
+                )
+
+        def multiply_all(a, m):
+            for s0, sn in spans(m):
+                for g in range(G):
+                    multiply(a, m, g, s0, sn)
+                if a == PASSES - 1:
+                    res = keep.tile([P, sn], F32, name="res%d_%d" % (m, s0))
+                    nc.scalar.activation(res[:], acc[(m, s0)][:], SILU, bias=bias[:, m : m + 1])
+                    nc.sync.dma_start(out[m * P : (m + 1) * P, s0 : s0 + sn], res[:])
+
+        gather_scales()
+        gather_both(0, "slot_plane")
+        interleave(0, 0, True, "g00")
+        quantize(0, 0)
+        multiply_all(0, 0)
+        gather_words(1, 0, 0, S, "g00")
+        interleave(0, 1, True, "g01")
+        quantize(0, 1)
+        multiply_all(0, 1)
+        gather_words(1, 1, 0, HALF, "g01")
+        interleave(0, 2, True, "g02")
+        quantize(0, 2)
+        multiply_all(0, 2)
+        gather_words(1, 1, HALF, HALF, "g02")
+        interleave(0, 3, True, "g03")
+        quantize(0, 3)
+        multiply_all(0, 3)
+        interleave(1, 0, True, "g10")
+        quantize(1, 0)
+        multiply_all(1, 0)
+        interleave(1, 1, True, "g11")
+        quantize(1, 1)
+        multiply_all(1, 1)
+        interleave(1, 2, False, "g03")
+        quantize(1, 2)
+        multiply_all(1, 2)
+        interleave(1, 3, False, "g10")
+        quantize(1, 3)
+        multiply_all(1, 3)

@@ -36,7 +36,7 @@ def tile_list_tabbag_silu_kernel(tc, tab, w, b, offs, out):
         nc.vector.memset(plane[:], 0)
         for q in range(4):
             lo = K_PASS * T + 4 * q * T
-            nc.scalar.dma_start(
+            nc.sync.dma_start(
                 plane[32 * q : 32 * q + 4 * PASSES, :],
                 tab[:, lo : lo + 4 * T].rearrange("a (r c) -> a r c", r=4).bitcast(I32),
             )
@@ -66,10 +66,10 @@ def tile_list_tabbag_silu_kernel(tc, tab, w, b, offs, out):
             with nc.allow_non_contiguous_dma(reason="one bias value a partition"):
                 nc.sync.dma_start(bias[:], b.rearrange("(m p) -> p m", p=P))
 
-        load_words(0)
         load_w(0, 0, 1)
-        load_words(1)
         load_bias()
+        load_words(0)
+        load_words(1)
         load_w(0, 1, 1)
         load_w(0, 2, 1)
         load_w(0, 3, 1)
@@ -96,8 +96,11 @@ def tile_list_tabbag_silu_kernel(tc, tab, w, b, offs, out):
 
         def gather_both(a, tag):
             t = keep.tile([P, G * S], U32, name="pw%d" % a, tag=tag, align_bytes=64)
-            nc.vector.tensor_copy(t[:], words[a][:].bitcast(U32).indirect(offsets[:]))
             for g in range(G):
+                nc.vector.tensor_copy(
+                    t[:, g * S : (g + 1) * S],
+                    words[a][:].bitcast(U32).indirect(offsets[:, g * LIST_COLS : (g + 1) * LIST_COLS]),
+                )
                 picked[(a, g)] = [(0, S, t[:, g * S : (g + 1) * S])]
 
         def gather_words(a, g, lo, n, tag):
@@ -154,10 +157,10 @@ def tile_list_tabbag_silu_kernel(tc, tab, w, b, offs, out):
                     nc.scalar.activation(res[:], acc[(m, s0)][:], SILU, bias=bias[:, m : m + 1])
                     nc.sync.dma_start(out[m * P : (m + 1) * P, s0 : s0 + sn], res[:])
 
-        gather_scales()
-        gather_both(0, "slot_plane")
         interleave(0, 0, True, "g00")
         quantize(0, 0)
+        gather_scales()
+        gather_both(0, "slot_plane")
         multiply_all(0, 0)
         gather_words(1, 0, 0, S, "g00")
         interleave(0, 1, True, "g01")

@@ -1,6 +1,7 @@
 from contextlib import ExitStack
 
 import concourse.mybir as mybir
+from concourse.masks import make_identity
 
 G, K, M, T, S = 2, 1024, 512, 2048, 512
 FLOPS = 2 * G * K * M * S
@@ -19,8 +20,8 @@ PACK = 4
 K_PASS = P * PACK
 PASSES = K // K_PASS
 TILES = M // P
-LIST_COLS = S // 16
 HALF = S // 2
+RES = {(0, 0): ("a", "raw0_3", 1536, 0), (0, 1): ("a", "raw0_3", 1536, 256), (1, 0): ("a", "raw0_3", 1536, 512), (1, 1): ("a", "raw0_3", 1536, 768), (2, 0): ("a", "raw0_3", 1536, 1024), (2, 1): ("a", "raw0_3", 1536, 1280), (3, 0): ("d", "rd", 256, 0), (3, 1): ("e", "re", 256, 0)}
 
 
 def tile_list_tabbag_silu_kernel(tc, tab, w, b, offs, out):
@@ -29,10 +30,10 @@ def tile_list_tabbag_silu_kernel(tc, tab, w, b, offs, out):
         keep = ctx.enter_context(tc.tile_pool(name="keep", bufs=1))
         psum = ctx.enter_context(tc.psum_pool(name="psum", bufs=1))
 
-        offsets = keep.tile([P, G * LIST_COLS], U16, name="offsets")
+        offsets = keep.tile([P, G * S // 16], U16, name="offsets")
         nc.sync.dma_start(offsets[:], offs)
 
-        plane = keep.tile([P, T // 4], I32, name="plane", tag="slot_plane", align_bytes=64)
+        plane = keep.tile([P, T // 4], I32, name="plane", tag="plane", align_bytes=64)
         nc.vector.memset(plane[:], 0)
         for q in range(4):
             lo = K_PASS * T + 4 * q * T
@@ -46,68 +47,45 @@ def tile_list_tabbag_silu_kernel(tc, tab, w, b, offs, out):
         nc.vector.memset(warm_in[:], 0.0)
         nc.scalar.activation(warm_out[:], warm_in[:], SILU)
 
-        words = {}
-        raw = {}
+        words, raw, picked, grouped, codes, scales, acc = {}, {}, {}, {}, {}, {}, {}
         bias = keep.tile([P, TILES], F32, name="bias")
+        picked_scales = keep.tile([P, G * S], U8, name="picked_scales", align_bytes=64)
 
         def load_words(a):
             wt = keep.tile([P, T], I32, name="words%d" % a, align_bytes=64)
             nc.sync.dma_start(wt[:], tab[a, 0 : K_PASS * T].rearrange("(p c) -> p c", p=P).bitcast(I32))
             words[a] = wt
 
-        def load_w(a, m0, n):
-            rt = keep.tile([P, PACK, n * P], F32, name="raw%d_%d" % (a, m0), align_bytes=64)
-            rows = w[a * K_PASS : (a + 1) * K_PASS, m0 * P : (m0 + n) * P]
-            nc.sync.dma_start(rt[:], rows.rearrange("(p j) c -> p j c", j=PACK))
+        def load_w(a, m0, n=1, pieces=1):
+            rt = keep.tile([P, PACK, n * P], F32, name="raw%d_%d" % (a, m0), tag="raw%d_%d" % (a, m0), align_bytes=64)
+            rows = w[a * K_PASS : (a + 1) * K_PASS, m0 * P : (m0 + n) * P].rearrange("(p j) c -> p j c", j=PACK)
+            step = PACK // pieces
+            for j in range(0, PACK, step):
+                nc.sync.dma_start(rt[:, j : j + step, :], rows[:, j : j + step, :])
             for i in range(n):
                 raw[(a, m0 + i)] = rt[:, :, i * P : (i + 1) * P]
 
         def load_bias():
-            with nc.allow_non_contiguous_dma(reason="one bias value a partition"):
-                nc.sync.dma_start(bias[:], b.rearrange("(m p) -> p m", p=P))
-
-        load_w(0, 0, 1)
-        load_bias()
-        load_words(0)
-        load_words(1)
-        load_w(0, 1, 1)
-        load_w(0, 2, 1)
-        load_w(0, 3, 1)
-        load_w(1, 0, 1)
-        load_w(1, 1, 1)
-        load_w(1, 2, 1)
-        load_w(1, 3, 1)
-
-        picked_scales = {}
-        picked = {}
-        grouped = {}
-        codes = {}
-        scales = {}
-        acc = {}
-        for m in range(TILES - 1):
-            acc[(m, 0)] = psum.tile([P, S], F32, name="acc%d" % m)
-        for lo in (0, HALF):
-            acc[(TILES - 1, lo)] = psum.tile([P, HALF], F32, name="acc_last%d" % lo)
+            ident = keep.tile([P, P], F32, name="ident")
+            make_identity(nc, ident[:])
+            rows = keep.tile([P, P], F32, name="bias_rows")
+            nc.vector.memset(rows[:], 0.0)
+            nc.sync.dma_start(rows[0:TILES, :], b.rearrange("(m p) -> m p", p=P))
+            turned = psum.tile([P, P], F32, name="bias_turned", tag="acc3_1")
+            nc.tensor.transpose(turned[:], rows[:], ident[:])
+            nc.scalar.copy(bias[:], turned[:, 0:TILES])
 
         def gather_scales():
-            t = keep.tile([P, G * S], U8, name="ps", align_bytes=64)
-            nc.vector.tensor_copy(t[:], plane[:].bitcast(U8).indirect(offsets[:]))
-            picked_scales[0] = t
+            nc.vector.tensor_copy(picked_scales[:], plane[:].bitcast(U8).indirect(offsets[:]))
 
-        def gather_both(a, tag):
-            t = keep.tile([P, G * S], U32, name="pw%d" % a, tag=tag, align_bytes=64)
-            for g in range(G):
-                nc.vector.tensor_copy(
-                    t[:, g * S : (g + 1) * S],
-                    words[a][:].bitcast(U32).indirect(offsets[:, g * LIST_COLS : (g + 1) * LIST_COLS]),
-                )
-                picked[(a, g)] = [(0, S, t[:, g * S : (g + 1) * S])]
-
-        def gather_words(a, g, lo, n, tag):
-            t = keep.tile([P, n], U32, name="pw%d_%d_%d" % (a, g, lo), tag=tag, align_bytes=64)
-            c0 = g * LIST_COLS + lo // 16
-            nc.vector.tensor_copy(t[:], words[a][:].bitcast(U32).indirect(offsets[:, c0 : c0 + n // 16]))
-            picked.setdefault((a, g), []).append((lo, n, t[:]))
+        def gather(a, g, h0, nh, tag, tile=None, at=0):
+            if tile is None:
+                tile = keep.tile([P, nh * HALF], U32, name="pw%d_%d_%d" % (a, g, h0), tag=tag, align_bytes=64)
+            c0 = (g * S + h0 * HALF) // 16
+            dst = tile[:, at : at + nh * HALF]
+            nc.vector.tensor_copy(dst, words[a][:].bitcast(U32).indirect(offsets[:, c0 : c0 + nh * HALF // 16]))
+            for i in range(nh):
+                picked[(a, g, h0 + i)] = dst[:, i * HALF : (i + 1) * HALF]
 
         def interleave(a, m, on_scalar, tag):
             t = keep.tile([P, P, PACK], BF16, name="gr%d_%d" % (a, m), tag=tag, align_bytes=64)
@@ -128,61 +106,96 @@ def tile_list_tabbag_silu_kernel(tc, tab, w, b, offs, out):
             codes[(a, m)] = c
             scales[(a, m)] = s
 
-        def spans(m):
-            return [(0, S)] if m < TILES - 1 else [(0, HALF), (HALF, HALF)]
+        done = {}
+        results = {}
 
-        def multiply(a, m, g, s0, sn):
-            parts = []
-            for lo, n, t in picked[(a, g)]:
-                x0, x1 = max(lo, s0), min(lo + n, s0 + sn)
-                if x1 > x0:
-                    parts.append((x0, x1, t[:, x0 - lo : x1 - lo]))
-            for i, (x0, x1, rhs) in enumerate(parts):
-                nc.tensor.matmul_mx(
-                    out=acc[(m, s0)][:, x0 - s0 : x1 - s0],
-                    lhsT=codes[(a, m)][:].bitcast(FP8X4),
-                    lhsT_scale=scales[(a, m)][:],
-                    rhs=rhs.bitcast(FP8X4),
-                    rhs_scale=picked_scales[0][4 * a : P, g * S + x0 : g * S + x1],
-                    start=(a == 0 and g == 0),
-                    stop=(a == PASSES - 1 and g == G - 1 and i == len(parts) - 1),
-                )
+        def multiply(a, m, g, h):
+            if (m, h) not in acc:
+                acc[(m, h)] = psum.tile([P, HALF], F32, name="acc%d_%d" % (m, h), tag="acc%d_%d" % (m, h))
+            n = done.get((m, h), 0)
+            done[(m, h)] = n + 1
+            x0 = g * S + h * HALF
+            nc.tensor.matmul_mx(
+                out=acc[(m, h)][:],
+                lhsT=codes[(a, m)][:].bitcast(FP8X4),
+                lhsT_scale=scales[(a, m)][:],
+                rhs=picked[(a, g, h)].bitcast(FP8X4),
+                rhs_scale=picked_scales[4 * a : P, x0 : x0 + HALF],
+                start=(n == 0),
+                stop=(n == PASSES * G - 1),
+            )
+            if n == PASSES * G - 1:
+                key, tag, width, at = RES[(m, h)]
+                if key not in results:
+                    results[key] = keep.tile([P, width], F32, name="res" + key, tag=tag, align_bytes=64)
+                res = results[key][:, at : at + HALF]
+                nc.scalar.activation(res, acc[(m, h)][:], SILU, bias=bias[:, m : m + 1])
+                queue = nc.scalar if (m, h) == (TILES - 1, 1) else nc.sync
+                queue.dma_start(out[m * P : (m + 1) * P, h * HALF : (h + 1) * HALF], res)
 
-        def multiply_all(a, m):
-            for s0, sn in spans(m):
-                for g in range(G):
-                    multiply(a, m, g, s0, sn)
-                if a == PASSES - 1:
-                    res = keep.tile([P, sn], F32, name="res%d_%d" % (m, s0))
-                    nc.scalar.activation(res[:], acc[(m, s0)][:], SILU, bias=bias[:, m : m + 1])
-                    nc.sync.dma_start(out[m * P : (m + 1) * P, s0 : s0 + sn], res[:])
+        load_w(0, 0, 1, 2)
+        load_words(0)
+        load_bias()
+        load_w(0, 1, 2)
+        load_words(1)
+        load_w(1, 0, 2)
+        load_w(1, 2)
+        load_w(0, 3)
+        load_w(1, 3)
 
         interleave(0, 0, True, "g00")
         quantize(0, 0)
         gather_scales()
-        gather_both(0, "slot_plane")
-        multiply_all(0, 0)
-        gather_words(1, 0, 0, S, "g00")
+        first = keep.tile([P, G * S], U32, name="pw0", tag="plane", align_bytes=64)
+        gather(0, 0, 0, 2, "", first, 0)
+        multiply(0, 0, 0, 0)
+        multiply(0, 0, 0, 1)
+        gather(0, 1, 0, 2, "", first, S)
+        multiply(0, 0, 1, 0)
+        multiply(0, 0, 1, 1)
         interleave(0, 1, True, "g01")
         quantize(0, 1)
-        multiply_all(0, 1)
-        gather_words(1, 1, 0, HALF, "g01")
+        multiply(0, 1, 0, 0)
+        multiply(0, 1, 1, 0)
+        multiply(0, 1, 0, 1)
+        multiply(0, 1, 1, 1)
         interleave(0, 2, True, "g02")
         quantize(0, 2)
-        multiply_all(0, 2)
-        gather_words(1, 1, HALF, HALF, "g02")
-        interleave(0, 3, True, "g03")
-        quantize(0, 3)
-        multiply_all(0, 3)
+        multiply(0, 2, 0, 0)
+        multiply(0, 2, 1, 0)
+        multiply(0, 2, 0, 1)
+        multiply(0, 2, 1, 1)
+        gather(1, 0, 0, 1, "pA")
+        gather(1, 1, 0, 1, "pB")
+        gather(1, 0, 1, 1, "pC")
         interleave(1, 0, True, "g10")
-        quantize(1, 0)
-        multiply_all(1, 0)
         interleave(1, 1, True, "g11")
+        interleave(1, 2, True, "g12")
+        interleave(0, 3, True, "g03")
+        quantize(1, 0)
+        multiply(1, 0, 0, 0)
+        multiply(1, 0, 1, 0)
         quantize(1, 1)
-        multiply_all(1, 1)
-        interleave(1, 2, False, "g03")
+        multiply(1, 1, 0, 0)
+        multiply(1, 1, 1, 0)
+        multiply(1, 0, 0, 1)
+        multiply(1, 1, 0, 1)
+        gather(1, 1, 1, 1, "g11")
+        multiply(1, 0, 1, 1)
+        multiply(1, 1, 1, 1)
         quantize(1, 2)
-        multiply_all(1, 2)
-        interleave(1, 3, False, "g10")
+        multiply(1, 2, 0, 0)
+        multiply(1, 2, 1, 0)
+        multiply(1, 2, 0, 1)
+        multiply(1, 2, 1, 1)
+        quantize(0, 3)
+        multiply(0, 3, 0, 0)
+        multiply(0, 3, 1, 0)
+        multiply(0, 3, 0, 1)
+        multiply(0, 3, 1, 1)
+        interleave(1, 3, False, "g13")
         quantize(1, 3)
-        multiply_all(1, 3)
+        multiply(1, 3, 0, 0)
+        multiply(1, 3, 1, 0)
+        multiply(1, 3, 0, 1)
+        multiply(1, 3, 1, 1)

from contextlib import ExitStack

import concourse.mybir as mybir
from concourse.masks import make_identity

G, K, M, T, S = 2, 1024, 512, 2048, 512
FLOPS = 2 * G * K * M * S

F32 = mybir.dt.float32
BF16 = mybir.dt.bfloat16
I32 = mybir.dt.int32
U32 = mybir.dt.uint32
U16 = mybir.dt.uint16
U8 = mybir.dt.uint8
FP8X4 = mybir.dt.float8_e4m3fn_x4
SILU = mybir.ActivationFunctionType.Silu

P = 128
PACK = 4
K_PASS = P * PACK
PASSES = K // K_PASS
TILES = M // P
HALF = S // 2
RES = {(0, 0): ("a", "raw0_3", 1536, 0), (0, 1): ("a", "raw0_3", 1536, 256), (1, 0): ("a", "raw0_3", 1536, 512), (1, 1): ("a", "raw0_3", 1536, 768), (2, 0): ("a", "raw0_3", 1536, 1024), (2, 1): ("a", "raw0_3", 1536, 1280), (3, 0): ("d", "rd", 256, 0), (3, 1): ("e", "re", 256, 0)}


def tile_list_tabbag_silu_kernel(tc, tab, w, b, offs, out):
    nc = tc.nc
    with ExitStack() as ctx:
        keep = ctx.enter_context(tc.tile_pool(name="keep", bufs=1))
        psum = ctx.enter_context(tc.psum_pool(name="psum", bufs=1))

        offsets = keep.tile([P, G * S // 16], U16, name="offsets")
        nc.sync.dma_start(offsets[:], offs)

        plane = keep.tile([P, T // 4], I32, name="plane", tag="plane", align_bytes=64)
        nc.vector.memset(plane[:], 0)
        for q in range(4):
            lo = K_PASS * T + 4 * q * T
            nc.sync.dma_start(
                plane[32 * q : 32 * q + 4 * PASSES, :],
                tab[:, lo : lo + 4 * T].rearrange("a (r c) -> a r c", r=4).bitcast(I32),
            )

        warm_in = keep.tile([P, 1], F32, name="warm_in")
        warm_out = keep.tile([P, 1], F32, name="warm_out")
        nc.vector.memset(warm_in[:], 0.0)
        nc.scalar.activation(warm_out[:], warm_in[:], SILU)

        words, raw, picked, grouped, codes, scales, acc = {}, {}, {}, {}, {}, {}, {}
        bias = keep.tile([P, TILES], F32, name="bias")
        picked_scales = keep.tile([P, G * S], U8, name="picked_scales", align_bytes=64)

        def load_words(a):
            wt = keep.tile([P, T], I32, name="words%d" % a, align_bytes=64)
            nc.sync.dma_start(wt[:], tab[a, 0 : K_PASS * T].rearrange("(p c) -> p c", p=P).bitcast(I32))
            words[a] = wt

        def load_w(a, m0, n=1, pieces=1):
            rt = keep.tile([P, PACK, n * P], F32, name="raw%d_%d" % (a, m0), tag="raw%d_%d" % (a, m0), align_bytes=64)
            rows = w[a * K_PASS : (a + 1) * K_PASS, m0 * P : (m0 + n) * P].rearrange("(p j) c -> p j c", j=PACK)
            step = PACK // pieces
            for j in range(0, PACK, step):
                nc.sync.dma_start(rt[:, j : j + step, :], rows[:, j : j + step, :])
            for i in range(n):
                raw[(a, m0 + i)] = rt[:, :, i * P : (i + 1) * P]

        def load_bias():
            ident = keep.tile([P, P], F32, name="ident")
            make_identity(nc, ident[:])
            rows = keep.tile([P, P], F32, name="bias_rows")
            nc.vector.memset(rows[:], 0.0)
            nc.sync.dma_start(rows[0:TILES, :], b.rearrange("(m p) -> m p", p=P))
            turned = psum.tile([P, P], F32, name="bias_turned", tag="acc3_1")
            nc.tensor.transpose(turned[:], rows[:], ident[:])
            nc.scalar.copy(bias[:], turned[:, 0:TILES])

        def gather_scales():
            nc.vector.tensor_copy(picked_scales[:], plane[:].bitcast(U8).indirect(offsets[:]))

        def gather(a, g, h0, nh, tag, tile=None, at=0):
            if tile is None:
                tile = keep.tile([P, nh * HALF], U32, name="pw%d_%d_%d" % (a, g, h0), tag=tag, align_bytes=64)
            c0 = (g * S + h0 * HALF) // 16
            dst = tile[:, at : at + nh * HALF]
            nc.vector.tensor_copy(dst, words[a][:].bitcast(U32).indirect(offsets[:, c0 : c0 + nh * HALF // 16]))
            for i in range(nh):
                picked[(a, g, h0 + i)] = dst[:, i * HALF : (i + 1) * HALF]

        def interleave(a, m, on_scalar, tag):
            t = keep.tile([P, P, PACK], BF16, name="gr%d_%d" % (a, m), tag=tag, align_bytes=64)
            dst = t[:].rearrange("p (c i) j -> p c j i", i=4)
            src = raw[(a, m)].rearrange("p j (c i) -> p c j i", i=4)
            if on_scalar:
                nc.scalar.copy(dst, src)
            else:
                nc.vector.tensor_copy(dst, src)
            grouped[(a, m)] = t

        def quantize(a, m):
            c = keep.tile([P, P], U32, name="wc%d_%d" % (a, m), align_bytes=64)
            s = keep.tile([P, P], U8, name="ws%d_%d" % (a, m), align_bytes=64)
            nc.vector.quantize_mx(
                out=c[:].bitcast(FP8X4), scales=s[:], in_=grouped[(a, m)][:].rearrange("p c j -> p (c j)")
            )
            codes[(a, m)] = c
            scales[(a, m)] = s

        done = {}
        results = {}

        def multiply(a, m, g, h):
            if (m, h) not in acc:
                acc[(m, h)] = psum.tile([P, HALF], F32, name="acc%d_%d" % (m, h), tag="acc%d_%d" % (m, h))
            n = done.get((m, h), 0)
            done[(m, h)] = n + 1
            x0 = g * S + h * HALF
            nc.tensor.matmul_mx(
                out=acc[(m, h)][:],
                lhsT=codes[(a, m)][:].bitcast(FP8X4),
                lhsT_scale=scales[(a, m)][:],
                rhs=picked[(a, g, h)].bitcast(FP8X4),
                rhs_scale=picked_scales[4 * a : P, x0 : x0 + HALF],
                start=(n == 0),
                stop=(n == PASSES * G - 1),
            )
            if n == PASSES * G - 1:
                key, tag, width, at = RES[(m, h)]
                if key not in results:
                    results[key] = keep.tile([P, width], F32, name="res" + key, tag=tag, align_bytes=64)
                res = results[key][:, at : at + HALF]
                nc.scalar.activation(res, acc[(m, h)][:], SILU, bias=bias[:, m : m + 1])
                queue = nc.scalar if (m, h) == (TILES - 1, 1) else nc.sync
                queue.dma_start(out[m * P : (m + 1) * P, h * HALF : (h + 1) * HALF], res)

        load_w(0, 0, 1, 2)
        load_words(0)
        load_bias()
        load_w(0, 1, 2)
        load_words(1)
        load_w(1, 0, 2)
        load_w(1, 2)
        load_w(0, 3)
        load_w(1, 3)

        interleave(0, 0, True, "g00")
        quantize(0, 0)
        gather_scales()
        first = keep.tile([P, G * S], U32, name="pw0", tag="plane", align_bytes=64)
        gather(0, 0, 0, 2, "", first, 0)
        multiply(0, 0, 0, 0)
        multiply(0, 0, 0, 1)
        gather(0, 1, 0, 2, "", first, S)
        multiply(0, 0, 1, 0)
        multiply(0, 0, 1, 1)
        interleave(0, 1, True, "g01")
        quantize(0, 1)
        multiply(0, 1, 0, 0)
        multiply(0, 1, 1, 0)
        multiply(0, 1, 0, 1)
        multiply(0, 1, 1, 1)
        interleave(0, 2, True, "g02")
        quantize(0, 2)
        multiply(0, 2, 0, 0)
        multiply(0, 2, 1, 0)
        multiply(0, 2, 0, 1)
        multiply(0, 2, 1, 1)
        gather(1, 0, 0, 1, "pA")
        gather(1, 1, 0, 1, "pB")
        gather(1, 0, 1, 1, "pC")
        interleave(1, 0, True, "g10")
        interleave(1, 1, True, "g11")
        interleave(1, 2, True, "g12")
        interleave(0, 3, True, "g03")
        quantize(1, 0)
        multiply(1, 0, 0, 0)
        multiply(1, 0, 1, 0)
        quantize(1, 1)
        multiply(1, 1, 0, 0)
        multiply(1, 1, 1, 0)
        multiply(1, 0, 0, 1)
        multiply(1, 1, 0, 1)
        gather(1, 1, 1, 1, "g11")
        multiply(1, 0, 1, 1)
        multiply(1, 1, 1, 1)
        quantize(1, 2)
        multiply(1, 2, 0, 0)
        multiply(1, 2, 1, 0)
        multiply(1, 2, 0, 1)
        multiply(1, 2, 1, 1)
        quantize(0, 3)
        multiply(0, 3, 0, 0)
        multiply(0, 3, 1, 0)
        multiply(0, 3, 0, 1)
        multiply(0, 3, 1, 1)
        interleave(1, 3, False, "g13")
        quantize(1, 3)
        multiply(1, 3, 0, 0)
        multiply(1, 3, 1, 0)
        multiply(1, 3, 0, 1)
        multiply(1, 3, 1, 1)
